import numpy as np
import ml_dtypes


def mxq(x, axis, fmt="e4m3"):
    dtype, down = {"e4m3": (ml_dtypes.float8_e4m3fn, 7), "e5m2": (ml_dtypes.float8_e5m2, 14)}[fmt]
    v = np.moveaxis(np.asarray(x, np.float32).astype(ml_dtypes.bfloat16).astype(np.float64), axis, -1)
    blocks = v.reshape(v.shape[:-1] + (-1, 32))
    amax = np.abs(blocks).max(-1, keepdims=True)
    byte = np.maximum(np.where(amax > 0, np.frexp(amax)[1] - 1 + 127, 0) - down, 1)
    scale = np.exp2(byte - 127.0)
    codes = (blocks / scale).astype(np.float32).astype(dtype).astype(np.float64)
    return np.moveaxis((codes * scale).reshape(v.shape), -1, axis)


WIDE = False


def mx_kscale(k):
    if not WIDE:
        return np.ones(k)
    levels = np.array([10, -10, 5, -5, 0])
    if k % 512:
        return np.exp2(np.random.permutation(np.resize(levels, k // 32))).repeat(32)
    a = np.empty((k // 512, 16))
    for p in range(k // 512):
        a[p, :8] = np.random.permutation(np.resize(levels, 8))
        for g in range(8):
            far = levels[np.abs(levels - a[p, g]) >= 10]
            a[p, g + 8] = far[np.random.randint(len(far))]
    return np.exp2(a.ravel()).repeat(32)


def f64(x):
    return np.asarray(x).astype(np.float64)


def striped(idx):
    return np.tile(idx.reshape(-1, 16).T, (8, 1)).astype(np.uint16)


def unstriped(offs):
    return offs[:16].T.reshape(-1).astype(np.int64)


def striped8(idx):
    return np.concatenate([x.reshape(-1, 16).T for x in idx]).astype(np.uint16)


def runs(offs, k):
    lists = np.stack([offs[16 * r : 16 * r + 16].T.reshape(-1) for r in range(8)]).astype(np.int64)
    return lists[np.arange(k) % 512 // 64]


def pack_weight(w):
    k, n = w.shape
    w = f64(np.asarray(w, np.float32).astype(ml_dtypes.bfloat16)).reshape(k // 32, 32, n)
    amax = np.abs(w).max(1)
    byte = np.clip(np.where(amax > 0, np.frexp(amax)[1] - 1 + 127 - 7, 1), 1, 254)
    scaled = (w * np.exp2(127.0 - byte)[:, None, :]).reshape(k, n).astype(np.float32)
    words = np.ascontiguousarray(scaled.reshape(k // 512, 128, 4, n).transpose(0, 1, 3, 2)).astype(ml_dtypes.float8_e4m3fn).view(np.uint8)
    return words, np.ascontiguousarray(byte.astype(np.uint8).reshape(k // 512, 16, n))


def unpack_weight(words, scales):
    g, p, n, _ = words.shape
    vals = np.ascontiguousarray(words).view(ml_dtypes.float8_e4m3fn).astype(np.float64) * np.repeat(np.exp2(scales.astype(np.float64) - 127.0), 8, axis=1)[..., None]
    return vals.transpose(0, 1, 3, 2).reshape(g * 512, n)


def sigmoid(v):
    return 1.0 / (1.0 + np.exp(-np.maximum(v, -700.0)))

def planes(y):
    n, m = y.shape
    v = y.astype(np.float32).astype(ml_dtypes.bfloat16).astype(np.float64).reshape(n // 32, 32, m)
    top = np.abs(v).max(1)
    byte = np.clip(np.where(top > 0, np.frexp(top)[1] - 1 + 127 - 7, 1), 1, 254)
    codes = (v * np.exp2(127.0 - byte)[:, None, :]).reshape(n, m).astype(np.float32).astype(ml_dtypes.float8_e4m3fn).view(np.uint8)
    words = codes.reshape(n // 512, 128, 4, m).transpose(0, 1, 3, 2)
    return np.ascontiguousarray(words), np.ascontiguousarray(byte.astype(np.uint8).reshape(n // 512, 16, m))


K, T, S, N, H, G, U = 512, 1024, 512, 512, 512, 2048, 1024


def setup_inputs():
    n = np.random.standard_normal
    s = mx_kscale(K)[:, None]
    u = mx_kscale(S)
    packed_xT = pack_weight(n((K, T)) * s)
    packed_w1 = pack_weight(n((K, H)) / np.sqrt(K) / s)
    packed_dT = pack_weight(n((K, G)) / s)
    packed_w2 = pack_weight(n((H, N)) / np.sqrt(H) / u[:, None])
    return {
        "x_words": packed_xT[0],
        "x_scales": packed_xT[1],
        "w1_words": packed_w1[0],
        "w1_scales": packed_w1[1],
        "gs": (np.random.uniform(0.5, 1.5, (K, 1)) * s).astype(np.float32),
        "d_words": packed_dT[0],
        "d_scales": packed_dT[1],
        "mem": n((H, U)).astype(np.float32),
        "res": (1.5 * n((N, U))).astype(np.float32),
        "gn": (np.random.uniform(0.5, 1.5, (H, 1)) * u[:, None]).astype(np.float32),
        "w2_words": packed_w2[0],
        "w2_scales": packed_w2[1],
        "offs": striped(np.random.permutation(T)[:S]),
        "n1": striped8(np.stack([np.random.permutation(S) for _ in range(8)])),
        "n2": striped8(np.stack([np.random.permutation(S) for _ in range(8)])),
        "kidx": striped8(np.random.randint(0, G, (8, H))),
        "n3": striped8(np.stack([np.random.permutation(U)[:S] for _ in range(8)])),
    }


def reference(x_words, x_scales, w1_words, w1_scales, gs, d_words, d_scales, mem, res, gn, w2_words, w2_scales, offs, n1, n2, kidx, n3):
    d_kidx = unpack_weight(d_words, d_scales)[np.arange(K)[:, None], runs(kidx, K)]
    xq = unpack_weight(x_words, x_scales)[:, unstriped(offs)]
    y = unpack_weight(w1_words, w1_scales).T @ xq
    z = f64(gs) * (y + (sigmoid(y[np.arange(H)[:, None], runs(n1, H)])) * (y[np.arange(H)[:, None], runs(n2, H)] - y))
    s = 0.0625 * ((d_kidx.T @ mxq(z, 0, "e4m3")))
    nw = np.maximum(s, 0.5 * (f64(mem)[np.arange(H)[:, None], runs(n3, H)]))
    pg = f64(mem).copy()
    pg[np.arange(H)[:, None], runs(n3, H)] = nw
    z2 = f64(gn) * pg
    out_0 = f64(res) + (unpack_weight(w2_words, w2_scales).T @ mxq(z2, 0, "e4m3"))
    return (out_0,) + planes(out_0)

@@ -1,0 +1,273 @@
+from contextlib import ExitStack
+
+import concourse.mybir as mybir
+
+K, T, S, N, H, G, U = 512, 1024, 512, 512, 512, 2048, 1024
+FLOPS = 2 * K * H * S + 2 * K * H * S + 2 * H * N * U
+
+F32 = mybir.dt.float32
+BF16 = mybir.dt.bfloat16
+I32 = mybir.dt.int32
+U32 = mybir.dt.uint32
+U16 = mybir.dt.uint16
+U8 = mybir.dt.uint8
+FP8X4 = mybir.dt.float8_e4m3fn_x4
+ALU = mybir.AluOpType
+ACT = mybir.ActivationFunctionType
+
+P = 128
+PACK = 4
+HALF = S // 2
+WIDTHS = (256, 256, 256, 128, 128)
+STAGED = 2
+
+
+def words_view(words):
+    return words[0].rearrange("p n t -> p (n t)").bitcast(I32)
+
+
+def deal(nc, dst, src, run):
+    nc.vector.tensor_copy(
+        out=dst.rearrange("p (t c i) -> p c t i", t=PACK, i=run),
+        in_=src.rearrange("p (c i t) -> p c t i", t=PACK, i=run),
+    )
+
+
+def tile_picked_pqktrackpagex_none_po_kernel(
+    tc, x_words, x_scales, w1_words, w1_scales, gs, d_words, d_scales, mem, res, gn, w2_words, w2_scales,
+    offs, n1, n2, kidx, n3, out_0, out_1, out_2,
+):
+    nc = tc.nc
+    with ExitStack() as ctx:
+        keep = ctx.enter_context(tc.tile_pool(name="keep", bufs=1))
+        psum = ctx.enter_context(tc.psum_pool(name="psum", bufs=8))
+
+        def sb(name, shape, dtype):
+            return keep.tile(shape, dtype, name=name, align_bytes=64)
+
+        def load_list(name, src):
+            lst = keep.tile([P, S // 16], U16, name=name)
+            nc.sync.dma_start(lst[:], src)
+            return lst
+
+        def scale_tile(name, width, engine):
+            plane = sb(name, [P, width], U8)
+            engine.memset(plane[:].bitcast(I32), 0)
+            return plane
+
+        def load_scales(queue, plane, scales, first_partition):
+            rows = scales[0].bitcast(I32)
+            for r in range(4):
+                queue.dma_start(plane[first_partition[r] : P : 32, :].bitcast(I32), rows[r:16:4, :])
+
+        xs = scale_tile("xs", T, nc.vector)
+        w1s = scale_tile("w1s", H, nc.vector)
+        ds = scale_tile("ds", G, nc.gpsimd)
+        w2s = scale_tile("w2s", N, nc.gpsimd)
+        key_s = scale_tile("key_s", H, nc.gpsimd)
+
+        offs_t = load_list("offs_t", offs)
+        xw = sb("xw", [P, T], I32)
+        nc.sync.dma_start(xw[:], words_view(x_words))
+        load_scales(nc.sync, xs, x_scales, (0, 1, 2, 3))
+        w1w = sb("w1w", [P, H], I32)
+        nc.sync.dma_start(w1w[:], words_view(w1_words))
+        load_scales(nc.sync, w1s, w1_scales, (0, 1, 2, 3))
+        n1_t = load_list("n1_t", n1)
+        gs_t = sb("gs_t", [P, PACK], F32)
+        nc.sync.dma_start(gs_t[:], gs.rearrange("(p t) o -> p (t o)", t=PACK))
+        n2_t = load_list("n2_t", n2)
+        kidx_t = load_list("kidx_t", kidx)
+        dw = sb("dw", [P, G], I32)
+        nc.sync.dma_start(dw[:], words_view(d_words))
+        load_scales(nc.sync, ds, d_scales, (0, 1, 16, 17))
+        n3_t = load_list("n3_t", n3)
+        mem_rows = mem.rearrange("(p t) w -> p t w", t=PACK)
+        page = []
+        for t in range(PACK):
+            page.append(sb("page%d" % t, [P, U], F32))
+            nc.sync.dma_start(page[t][:], mem_rows[:, t, :])
+        gn_t = sb("gn_t", [P, PACK], F32)
+        nc.sync.dma_start(gn_t[:], gn.rearrange("(p t) o -> p (t o)", t=PACK))
+        w2w = sb("w2w", [P, N], I32)
+        nc.sync.dma_start(w2w[:], words_view(w2_words))
+        load_scales(nc.sync, w2s, w2_scales, (0, 1, 2, 3))
+        res_rows = res.rearrange("(p t) w -> p t w", t=PACK)
+        res_t = sb("res_t", [P, PACK, U], F32)
+        nc.sync.dma_start(res_t[:], res_rows)
+
+        warm = sb("warm", [P, 8], F32)
+        warm_in = sb("warm_in", [P, 8], F32)
+        nc.gpsimd.memset(warm_in[:], 0.0)
+        nc.scalar.activation(warm[:], warm_in[:], ACT.Sigmoid)
+
+        xq_s = sb("xq_s", [P, S], U8)
+        nc.vector.tensor_copy(xq_s[:], xs[:].indirect(offs_t[:]))
+        xq_w = sb("xq_w", [P, S], U32)
+        nc.vector.tensor_copy(xq_w[:], xw[:].bitcast(U32).indirect(offs_t[:]))
+        w1w_d = sb("w1w_d", [P, H], I32)
+        deal(nc, w1w_d[:], w1w[:], 4)
+        w1s_d = sb("w1s_d", [P, H], U8)
+        deal(nc, w1s_d[:], w1s[:], 16)
+
+        def product(bank, lw, ls, t, rw, rs):
+            cols = slice(t * P, (t + 1) * P)
+            nc.tensor.matmul_mx(out=bank, lhsT=lw[:, cols].bitcast(FP8X4), lhsT_scale=ls[:, cols],
+                                rhs=rw.bitcast(FP8X4), rhs_scale=rs, start=True, stop=True)
+
+        y_banks = []
+        for t in range(PACK):
+            bank = psum.tile([P, S], F32, name="bank")
+            product(bank[:], w1w_d, w1s_d, t, xq_w[:], xq_s[:])
+            y_banks.append(bank)
+
+        key_w_g = sb("key_w_g", [P, H], U32)
+        nc.vector.tensor_copy(key_w_g[:], dw[:].bitcast(U32).indirect(kidx_t[:]))
+        key_s_g = sb("key_s_g", [P, H], U8)
+        nc.vector.tensor_copy(key_s_g[:], ds[:].indirect(kidx_t[:]))
+        key_s_d = sb("key_s_d", [P, H], U8)
+        deal(nc, key_s_d[:], key_s_g[:], 16)
+        key_w = sb("key_w", [P, H], I32)
+        deal(nc, key_w[:], key_w_g[:].bitcast(I32), 4)
+        for r, src in enumerate((0, 1, 16, 17)):
+            nc.scalar.dma_start(key_s[r:P:32, :].bitcast(I32), key_s_d[src:P:32, :].bitcast(I32))
+
+        far = sb("far", [P, PACK, S], F32)
+        near = sb("near", [P, PACK, S], F32)
+        for t in range(PACK):
+            y = sb("y%d" % t, [P, S], F32)
+            nc.scalar.copy(y[:], y_banks[t][:])
+            gate = sb("gate%d" % t, [P, S], F32)
+            for h in range(2):
+                nc.scalar.activation(gate[:, h * HALF : (h + 1) * HALF], y[:].indirect(n1_t[:, h * 16 : (h + 1) * 16]), ACT.Sigmoid)
+            a = sb("a%d" % t, [P, S], F32)
+            nc.scalar.activation(a[:], y_banks[t][:], ACT.Copy, scale=gs_t[:, t : t + 1])
+            for h in range(2):
+                cols = slice(h * HALF, (h + 1) * HALF)
+                nc.vector.tensor_tensor(far[:, t, cols], a[:].indirect(n2_t[:, h * 16 : (h + 1) * 16]), gate[:, cols], ALU.mult)
+            nc.vector.scalar_tensor_tensor(near[:, t, :], gate[:], 1.0, a[:], ALU.subtract, ALU.mult)
+
+        z = sb("z", [P, S * PACK], BF16)
+        z_w = sb("z_w", [P, S], U32)
+        z_s = sb("z_s", [P, S], U8)
+        for h in range(2):
+            cols = slice(h * HALF, (h + 1) * HALF)
+            wide = slice(h * HALF * PACK, (h + 1) * HALF * PACK)
+            nc.vector.tensor_tensor(
+                z[:, wide].rearrange("p (c i t) -> p c t i", t=PACK, i=4),
+                far[:, :, cols].rearrange("p t (c i) -> p c t i", i=4),
+                near[:, :, cols].rearrange("p t (c i) -> p c t i", i=4),
+                ALU.subtract,
+            )
+        old = [sb("old%d" % t, [P, S], F32) for t in range(PACK)]
+        new = [sb("new%d" % t, [P, S], F32) for t in range(PACK)]
+
+        def fetch_old(t):
+            nc.vector.tensor_scalar(old[t][:], page[t][:].indirect(n3_t[:]), 0.5, 0.0, ALU.mult, ALU.add)
+
+        fetch_old(0)
+        nc.vector.quantize_mx(out=z_w[:].bitcast(FP8X4), scales=z_s[:], in_=z[:])
+        s_banks = []
+        for t in range(PACK):
+            bank = psum.tile([P, S], F32, name="bank")
+            product(bank[:], key_w, key_s, t, z_w[:], z_s[:])
+            s_banks.append(bank)
+        fetch_old(1)
+
+        chunks = []
+        start = 0
+        for width in WIDTHS:
+            chunks.append(slice(start, start + width))
+            start = start + width
+        z2 = [sb("z2_%d" % c, [P, width * PACK], BF16) for c, width in enumerate(WIDTHS)]
+        staged = sum(WIDTHS[:STAGED])
+        z2_planes = sb("z2_planes", [P, PACK, staged], BF16)
+
+        def larger(t):
+            nc.vector.scalar_tensor_tensor(new[t][:], s_banks[t][:], 0.0625, old[t][:], ALU.mult, ALU.max)
+
+        def put(t):
+            nc.vector.tensor_copy(page[t][:].indirect(n3_t[:]), new[t][:])
+            for c, cols in enumerate(chunks):
+                if c < STAGED:
+                    dst = z2_planes[:, t, cols]
+                else:
+                    dst = z2[c][:].rearrange("p (w t) -> p t w", t=PACK)[:, t, :]
+                nc.scalar.activation(dst, page[t][:, cols], ACT.Copy, scale=gn_t[:, t : t + 1])
+
+        larger(0)
+        fetch_old(2)
+        put(0)
+        larger(1)
+        fetch_old(3)
+        put(1)
+        larger(2)
+        w2w_d = sb("w2w_d", [P, N], I32)
+        deal(nc, w2w_d[:], w2w[:], 4)
+        put(2)
+        larger(3)
+        w2s_d = sb("w2s_d", [P, N], U8)
+        deal(nc, w2s_d[:], w2s[:], 16)
+        put(3)
+
+        out_rows = out_0.rearrange("(p t) w -> p t w", t=PACK)
+        out_words = words_view(out_1)
+        out_s = sb("out_s", [P, U], U8)
+        banks = {}
+        rounded = {}
+
+        def weave(c):
+            if c < STAGED:
+                nc.vector.tensor_copy(
+                    z2[c][:].rearrange("p (c i t) -> p c t i", t=PACK, i=4),
+                    z2_planes[:, :, chunks[c]].rearrange("p t (c i) -> p c t i", i=4),
+                )
+
+        def multiply(c):
+            width = WIDTHS[c]
+            z2_w = sb("z2_w%d" % c, [P, width], U32)
+            z2_s = sb("z2_s%d" % c, [P, width], U8)
+            nc.vector.quantize_mx(out=z2_w[:].bitcast(FP8X4), scales=z2_s[:], in_=z2[c][:])
+            per_bank = 512 // width
+            banks[c] = []
+            for b in range(PACK // per_bank):
+                bank = psum.tile([P, per_bank, width], F32, name="bank")
+                for u in range(per_bank):
+                    product(bank[:, u, :], w2w_d, w2s_d, per_bank * b + u, z2_w[:], z2_s[:])
+                banks[c].append(bank)
+
+        def finish(c):
+            width = WIDTHS[c]
+            cols = chunks[c]
+            per_bank = 512 // width
+            result = sb("result%d" % c, [P, PACK, width], F32)
+            for b, bank in enumerate(banks[c]):
+                planes = slice(per_bank * b, per_bank * (b + 1))
+                nc.vector.tensor_tensor(result[:, planes, :], bank[:], res_t[:, planes, cols], ALU.add)
+            nc.sync.dma_start(out_rows[:, :, cols], result[:])
+            rounded[c] = sb("rounded%d" % c, [P, width * PACK], BF16)
+            nc.scalar.copy(
+                rounded[c][:].rearrange("p (c i t) -> p c t i", t=PACK, i=4),
+                result[:].rearrange("p t (c i) -> p c t i", i=4),
+            )
+
+        def hand_on(c):
+            out_w = sb("out_w%d" % c, [P, WIDTHS[c]], I32)
+            nc.vector.quantize_mx(out=out_w[:].bitcast(FP8X4), scales=out_s[:, chunks[c]], in_=rounded[c][:])
+            nc.sync.dma_start(out_words[:, chunks[c]], out_w[:])
+
+        count = len(WIDTHS)
+        weave(0)
+        for step in range(count + 2):
+            if step + 1 < count:
+                weave(step + 1)
+            if step < count:
+                multiply(step)
+            if 0 <= step - 1 < count:
+                finish(step - 1)
+            if 0 <= step - 2 < count:
+                hand_on(step - 2)
+        scale_rows = out_2[0].bitcast(I32)
+        for q in range(4):
+            queue = nc.sync if q % 2 == 0 else nc.scalar
+            queue.dma_start(scale_rows[4 * q : 4 * q + 4, :], out_s[32 * q : 32 * q + 4, :].bitcast(I32))

@@ -26,8 +26,8 @@ def words_view(words):
     return words[0].rearrange("p n t -> p (n t)").bitcast(I32)
 
 
-def deal(nc, dst, src, run):
-    nc.vector.tensor_copy(
+def deal(engine, dst, src, run):
+    engine.tensor_copy(
         out=dst.rearrange("p (t c i) -> p c t i", t=PACK, i=run),
         in_=src.rearrange("p (c i t) -> p c t i", t=PACK, i=run),
     )
@@ -40,6 +40,7 @@ def tile_picked_pqktrackpagex_none_po_kernel(
     nc = tc.nc
     with ExitStack() as ctx:
         keep = ctx.enter_context(tc.tile_pool(name="keep", bufs=1))
+        ring = ctx.enter_context(tc.tile_pool(name="ring", bufs=4))
         psum = ctx.enter_context(tc.psum_pool(name="psum", bufs=8))
 
         def sb(name, shape, dtype):
@@ -63,8 +64,9 @@ def tile_picked_pqktrackpagex_none_po_kernel(
         xs = scale_tile("xs", T, nc.vector)
         w1s = scale_tile("w1s", H, nc.vector)
         ds = scale_tile("ds", G, nc.gpsimd)
-        w2s = scale_tile("w2s", N, nc.gpsimd)
-        key_s = scale_tile("key_s", H, nc.gpsimd)
+        load_scales(nc.gpsimd, ds, d_scales, (0, 1, 16, 17))
+        key_s = scale_tile("key_s", H, nc.vector)
+        w2s = scale_tile("w2s", N, nc.vector)
 
         offs_t = load_list("offs_t", offs)
         xw = sb("xw", [P, T], I32)
@@ -74,27 +76,16 @@ def tile_picked_pqktrackpagex_none_po_kernel(
         nc.sync.dma_start(w1w[:], words_view(w1_words))
         load_scales(nc.sync, w1s, w1_scales, (0, 1, 2, 3))
         n1_t = load_list("n1_t", n1)
+        kidx_t = load_list("kidx_t", kidx)
         gs_t = sb("gs_t", [P, PACK], F32)
         nc.sync.dma_start(gs_t[:], gs.rearrange("(p t) o -> p (t o)", t=PACK))
         n2_t = load_list("n2_t", n2)
-        kidx_t = load_list("kidx_t", kidx)
         dw = sb("dw", [P, G], I32)
         nc.sync.dma_start(dw[:], words_view(d_words))
-        load_scales(nc.sync, ds, d_scales, (0, 1, 16, 17))
         n3_t = load_list("n3_t", n3)
-        mem_rows = mem.rearrange("(p t) w -> p t w", t=PACK)
-        page = []
-        for t in range(PACK):
-            page.append(sb("page%d" % t, [P, U], F32))
-            nc.sync.dma_start(page[t][:], mem_rows[:, t, :])
         gn_t = sb("gn_t", [P, PACK], F32)
         nc.sync.dma_start(gn_t[:], gn.rearrange("(p t) o -> p (t o)", t=PACK))
-        w2w = sb("w2w", [P, N], I32)
-        nc.sync.dma_start(w2w[:], words_view(w2_words))
         load_scales(nc.sync, w2s, w2_scales, (0, 1, 2, 3))
-        res_rows = res.rearrange("(p t) w -> p t w", t=PACK)
-        res_t = sb("res_t", [P, PACK, U], F32)
-        nc.sync.dma_start(res_t[:], res_rows)
 
         warm = sb("warm", [P, 8], F32)
         warm_in = sb("warm_in", [P, 8], F32)
@@ -106,9 +97,15 @@ def tile_picked_pqktrackpagex_none_po_kernel(
         xq_w = sb("xq_w", [P, S], U32)
         nc.vector.tensor_copy(xq_w[:], xw[:].bitcast(U32).indirect(offs_t[:]))
         w1w_d = sb("w1w_d", [P, H], I32)
-        deal(nc, w1w_d[:], w1w[:], 4)
+        deal(nc.vector, w1w_d[:], w1w[:], 4)
         w1s_d = sb("w1s_d", [P, H], U8)
-        deal(nc, w1s_d[:], w1s[:], 16)
+        deal(nc.vector, w1s_d[:], w1s[:], 16)
+
+        mem_rows = mem.rearrange("(p t) w -> p t w", t=PACK)
+        page = []
+        for t, freed in enumerate(("xs", "xw", "w1w", "w1s")):
+            page.append(sb(freed, [P, U], F32))
+            nc.sync.dma_start(page[t][:], mem_rows[:, t, :])
 
         def product(bank, lw, ls, t, rw, rs):
             cols = slice(t * P, (t + 1) * P)
@@ -121,58 +118,87 @@ def tile_picked_pqktrackpagex_none_po_kernel(
             product(bank[:], w1w_d, w1s_d, t, xq_w[:], xq_s[:])
             y_banks.append(bank)
 
-        key_w_g = sb("key_w_g", [P, H], U32)
-        nc.vector.tensor_copy(key_w_g[:], dw[:].bitcast(U32).indirect(kidx_t[:]))
+        y = [sb("y%d" % t, [P, S], F32) for t in range(PACK)]
+        z = [sb("z%d" % h, [P, HALF * PACK], BF16) for h in range(2)]
+        z_w = sb("z_w", [P, S], U32)
+        z_s = sb("z_s", [P, S], U8)
+        halves = [slice(h * HALF, (h + 1) * HALF) for h in range(2)]
+        entries = [slice(h * HALF // 16, (h + 1) * HALF // 16) for h in range(2)]
+
+        a = [sb("a%d" % t, [P, S], F32) for t in range(PACK)]
+        gate = [[sb("gate%d_%d" % (h, t), [P, HALF], F32) for t in range(PACK)] for h in range(2)]
+        far = sb("far", [P, PACK, HALF], F32)
+        near = sb("near", [P, PACK, HALF], F32)
+
+        def make_gate(t, h):
+            nc.scalar.activation(gate[h][t][:], y[t][:].indirect(n1_t[:, entries[h]]), ACT.Sigmoid)
+
+        for t in range(PACK):
+            nc.scalar.copy(y[t][:], y_banks[t][:])
+            make_gate(t, 0)
+            nc.scalar.activation(a[t][:], y_banks[t][:], ACT.Copy, scale=gs_t[:, t : t + 1])
+            nc.vector.tensor_tensor(far[:, t, :], a[t][:].indirect(n2_t[:, entries[0]]), gate[0][t][:], ALU.mult)
+            nc.vector.scalar_tensor_tensor(near[:, t, :], gate[0][t][:], 1.0, a[t][:, halves[0]], ALU.subtract, ALU.mult)
+
         key_s_g = sb("key_s_g", [P, H], U8)
         nc.vector.tensor_copy(key_s_g[:], ds[:].indirect(kidx_t[:]))
         key_s_d = sb("key_s_d", [P, H], U8)
-        deal(nc, key_s_d[:], key_s_g[:], 16)
+        deal(nc.vector, key_s_d[:], key_s_g[:], 16)
+        key_w_g = sb("key_w_g", [P, H], U32)
+        nc.vector.tensor_copy(key_w_g[:], dw[:].bitcast(U32).indirect(kidx_t[:]))
         key_w = sb("key_w", [P, H], I32)
-        deal(nc, key_w[:], key_w_g[:].bitcast(I32), 4)
+        deal(nc.vector, key_w[:], key_w_g[:].bitcast(I32), 4)
         for r, src in enumerate((0, 1, 16, 17)):
-            nc.scalar.dma_start(key_s[r:P:32, :].bitcast(I32), key_s_d[src:P:32, :].bitcast(I32))
+            nc.gpsimd.dma_start(key_s[r:P:32, :].bitcast(I32), key_s_d[src:P:32, :].bitcast(I32))
 
-        far = sb("far", [P, PACK, S], F32)
-        near = sb("near", [P, PACK, S], F32)
+        w2w = sb("ds", [P, N], I32)
+        nc.sync.dma_start(w2w[:], words_view(w2_words))
+        res_t = sb("dw", [P, PACK, U], F32)
+        nc.sync.dma_start(res_t[:], res.rearrange("(p t) w -> p t w", t=PACK))
+
         for t in range(PACK):
-            y = sb("y%d" % t, [P, S], F32)
-            nc.scalar.copy(y[:], y_banks[t][:])
-            gate = sb("gate%d" % t, [P, S], F32)
-            for h in range(2):
-                nc.scalar.activation(gate[:, h * HALF : (h + 1) * HALF], y[:].indirect(n1_t[:, h * 16 : (h + 1) * 16]), ACT.Sigmoid)
-            a = sb("a%d" % t, [P, S], F32)
-            nc.scalar.activation(a[:], y_banks[t][:], ACT.Copy, scale=gs_t[:, t : t + 1])
-            for h in range(2):
-                cols = slice(h * HALF, (h + 1) * HALF)
-                nc.vector.tensor_tensor(far[:, t, cols], a[:].indirect(n2_t[:, h * 16 : (h + 1) * 16]), gate[:, cols], ALU.mult)
-            nc.vector.scalar_tensor_tensor(near[:, t, :], gate[:], 1.0, a[:], ALU.subtract, ALU.mult)
+            make_gate(t, 1)
+        nc.vector.tensor_tensor(
+            z[0][:].rearrange("p (c i t) -> p c t i", t=PACK, i=4),
+            far[:].rearrange("p t (c i) -> p c t i", i=4),
+            near[:].rearrange("p t (c i) -> p c t i", i=4),
+            ALU.subtract,
+        )
 
-        z = sb("z", [P, S * PACK], BF16)
-        z_w = sb("z_w", [P, S], U32)
-        z_s = sb("z_s", [P, S], U8)
-        for h in range(2):
-            cols = slice(h * HALF, (h + 1) * HALF)
-            wide = slice(h * HALF * PACK, (h + 1) * HALF * PACK)
-            nc.vector.tensor_tensor(
-                z[:, wide].rearrange("p (c i t) -> p c t i", t=PACK, i=4),
-                far[:, :, cols].rearrange("p t (c i) -> p c t i", i=4),
-                near[:, :, cols].rearrange("p t (c i) -> p c t i", i=4),
-                ALU.subtract,
-            )
-        old = [sb("old%d" % t, [P, S], F32) for t in range(PACK)]
+        old_first = sb("old_first", [P, S], F32)
+        old_rest = sb("near", [P, PACK - 1, S], F32)
+        old = [old_first[:]] + [old_rest[:, t, :] for t in range(PACK - 1)]
         new = [sb("new%d" % t, [P, S], F32) for t in range(PACK)]
+        s_banks = [psum.tile([P, S], F32, name="bank") for t in range(PACK)]
 
-        def fetch_old(t):
-            nc.vector.tensor_scalar(old[t][:], page[t][:].indirect(n3_t[:]), 0.5, 0.0, ALU.mult, ALU.add)
+        def quantise_z(h):
+            nc.vector.quantize_mx(out=z_w[:, halves[h]].bitcast(FP8X4), scales=z_s[:, halves[h]], in_=z[h][:])
 
-        fetch_old(0)
-        nc.vector.quantize_mx(out=z_w[:].bitcast(FP8X4), scales=z_s[:], in_=z[:])
-        s_banks = []
+        def score(t, cols):
+            product(s_banks[t][:, cols], key_w, key_s, t, z_w[:, cols], z_s[:, cols])
+
+        last = PACK - 1
         for t in range(PACK):
-            bank = psum.tile([P, S], F32, name="bank")
-            product(bank[:], key_w, key_s, t, z_w[:], z_s[:])
-            s_banks.append(bank)
-        fetch_old(1)
+            nc.vector.tensor_copy(far[:, t, :], a[t][:].indirect(n2_t[:, entries[1]]))
+            if t == 0:
+                quantise_z(0)
+                for u in range(last):
+                    score(u, halves[0])
+
+        for pair in ((0, 1), (2, 3)):
+            step = {t: ring.tile([P, HALF], F32, name="step") for t in pair}
+            pull = {t: ring.tile([P, HALF], F32, name="pull") for t in pair}
+            mixed = {t: ring.tile([P, HALF], F32, name="mixed") for t in pair}
+            for t in pair:
+                nc.gpsimd.tensor_tensor(step[t][:], far[:, t, :], a[t][:, halves[1]], ALU.subtract)
+            for t in pair:
+                nc.gpsimd.tensor_tensor(pull[t][:], step[t][:], gate[1][t][:], ALU.mult)
+            for t in pair:
+                nc.gpsimd.tensor_tensor(mixed[t][:], pull[t][:], a[t][:, halves[1]], ALU.add)
+                nc.scalar.copy(z[1][:].rearrange("p (j t) -> p t j", t=PACK)[:, t, :], mixed[t][:])
+
+        for t in range(PACK):
+            nc.vector.tensor_scalar(old[t], page[t][:].indirect(n3_t[:]), 0.5, 0.0, ALU.mult, ALU.add)
 
         chunks = []
         start = 0
@@ -183,11 +209,13 @@ def tile_picked_pqktrackpagex_none_po_kernel(
         staged = sum(WIDTHS[:STAGED])
         z2_planes = sb("z2_planes", [P, PACK, staged], BF16)
 
-        def larger(t):
-            nc.vector.scalar_tensor_tensor(new[t][:], s_banks[t][:], 0.0625, old[t][:], ALU.mult, ALU.max)
+        def larger(t, cols):
+            nc.vector.scalar_tensor_tensor(new[t][:, cols], s_banks[t][:, cols], 0.0625, old[t][:, cols], ALU.mult, ALU.max)
 
-        def put(t):
-            nc.vector.tensor_copy(page[t][:].indirect(n3_t[:]), new[t][:])
+        def put(t, cols):
+            nc.vector.tensor_copy(page[t][:].indirect(n3_t[:, cols.start // 16 : cols.stop // 16]), new[t][:, cols])
+
+        def weigh(t):
             for c, cols in enumerate(chunks):
                 if c < STAGED:
                     dst = z2_planes[:, t, cols]
@@ -195,21 +223,31 @@ def tile_picked_pqktrackpagex_none_po_kernel(
                     dst = z2[c][:].rearrange("p (w t) -> p t w", t=PACK)[:, t, :]
                 nc.scalar.activation(dst, page[t][:, cols], ACT.Copy, scale=gn_t[:, t : t + 1])
 
-        larger(0)
-        fetch_old(2)
-        put(0)
-        larger(1)
-        fetch_old(3)
-        put(1)
-        larger(2)
-        w2w_d = sb("w2w_d", [P, N], I32)
-        deal(nc, w2w_d[:], w2w[:], 4)
-        put(2)
-        larger(3)
-        w2s_d = sb("w2s_d", [P, N], U8)
-        deal(nc, w2s_d[:], w2s[:], 16)
-        put(3)
+        whole = slice(0, S)
+        for h in range(2):
+            pieces = [(t, halves[h]) for t in range(last)]
+            if h == 1:
+                pieces.append((last, whole))
+            larger(*pieces[0])
+            for n, (t, cols) in enumerate(pieces):
+                if n + 1 < len(pieces):
+                    larger(*pieces[n + 1])
+                elif h == 0:
+                    quantise_z(1)
+                    for u in range(last):
+                        score(u, halves[1])
+                    score(last, whole)
+                put(t, cols)
+                if h == 1:
+                    weigh(t)
 
+        w2w_d = sb("a3", [P, N], I32)
+        deal(nc.gpsimd, w2w_d[:], w2w[:], 4)
+        w2s_d = sb("a2", [P, N], U8)
+        deal(nc.gpsimd, w2s_d[:], w2s[:], 16)
+
+        probe = sb("probe", [P, 8], F32)
+        nc.gpsimd.tensor_copy(probe[:, 0:1], page[3][:, 0:1])
         out_rows = out_0.rearrange("(p t) w -> p t w", t=PACK)
         out_words = words_view(out_1)
         out_s = sb("out_s", [P, U], U8)

@@ -16,21 +16,46 @@ ALU = mybir.AluOpType
 ACT = mybir.ActivationFunctionType
 
 P = 128
-PACK = 4
+PLANES = 4
+GROUP = 16
+QUADRANT = 32
+BANK = 512
+LINE = 16
 HALF = S // 2
 WIDTHS = (256, 256, 256, 128, 128)
-STAGED = 2
+WOVEN = 2
+SCALE_ROWS = (0, 1, 2, 3)
+KEY_SCALE_ROWS = (0, 1, GROUP, GROUP + 1)
 
 
 def words_view(words):
     return words[0].rearrange("p n t -> p (n t)").bitcast(I32)
 
 
-def deal(engine, dst, src, run):
+def planes_view(rows):
+    return rows.rearrange("(p t) w -> p t w", t=PLANES)
+
+
+def deal(engine, dst, src, per_line):
     engine.tensor_copy(
-        out=dst.rearrange("p (t c i) -> p c t i", t=PACK, i=run),
-        in_=src.rearrange("p (c i t) -> p c t i", t=PACK, i=run),
+        out=dst.rearrange("p (t c i) -> p c t i", t=PLANES, i=per_line),
+        in_=src.rearrange("p (c i t) -> p c t i", t=PLANES, i=per_line),
     )
+
+
+def interleave(copy, dst, src):
+    copy(
+        dst.rearrange("p (c i t) -> p c t i", t=PLANES, i=4),
+        src.rearrange("p t (c i) -> p c t i", i=4),
+    )
+
+
+def plane_of(interleaved, t):
+    return interleaved[:].rearrange("p (c t) -> p t c", t=PLANES)[:, t, :]
+
+
+def entries(lists, cols):
+    return lists[:, cols.start // GROUP : cols.stop // GROUP]
 
 
 def tile_picked_pqktrackpagex_none_po_kernel(
@@ -40,151 +65,144 @@ def tile_picked_pqktrackpagex_none_po_kernel(
     nc = tc.nc
     with ExitStack() as ctx:
         keep = ctx.enter_context(tc.tile_pool(name="keep", bufs=1))
-        ring = ctx.enter_context(tc.tile_pool(name="ring", bufs=4))
+        ring = ctx.enter_context(tc.tile_pool(name="ring", bufs=PLANES))
         psum = ctx.enter_context(tc.psum_pool(name="psum", bufs=8))
 
-        def sb(name, shape, dtype):
-            return keep.tile(shape, dtype, name=name, align_bytes=64)
+        def sb(name, shape, dtype, after=None):
+            return keep.tile(shape, dtype, name=name, tag=after or name, align_bytes=64)
 
         def load_list(name, src):
-            lst = keep.tile([P, S // 16], U16, name=name)
-            nc.sync.dma_start(lst[:], src)
-            return lst
+            lists = keep.tile([P, S // GROUP], U16, name=name)
+            nc.sync.dma_start(lists[:], src)
+            return lists
+
+        def load_words(name, src, width, after=None):
+            words = sb(name, [P, width], I32, after)
+            nc.sync.dma_start(words[:], words_view(src))
+            return words
+
+        def load_gain(name, src):
+            gain = sb(name, [P, PLANES], F32)
+            nc.sync.dma_start(gain[:], src.rearrange("(p t) o -> p (t o)", t=PLANES))
+            return gain
 
         def scale_tile(name, width, engine):
-            plane = sb(name, [P, width], U8)
-            engine.memset(plane[:].bitcast(I32), 0)
-            return plane
+            scales = sb(name, [P, width], U8)
+            engine.memset(scales[:].bitcast(I32), 0)
+            return scales
 
-        def load_scales(queue, plane, scales, first_partition):
-            rows = scales[0].bitcast(I32)
-            for r in range(4):
-                queue.dma_start(plane[first_partition[r] : P : 32, :].bitcast(I32), rows[r:16:4, :])
+        def load_scales(queue, scales, src, first_partitions):
+            rows = src[0].bitcast(I32)
+            for r, first in enumerate(first_partitions):
+                queue.dma_start(scales[first:P:QUADRANT, :].bitcast(I32), rows[r :: len(first_partitions), :])
 
-        xs = scale_tile("xs", T, nc.vector)
-        w1s = scale_tile("w1s", H, nc.vector)
-        ds = scale_tile("ds", G, nc.gpsimd)
-        load_scales(nc.gpsimd, ds, d_scales, (0, 1, 16, 17))
+        def product(bank, lhs_words, lhs_scales, t, rhs_words, rhs_scales):
+            cols = slice(t * P, (t + 1) * P)
+            nc.tensor.matmul_mx(
+                out=bank, lhsT=lhs_words[:, cols].bitcast(FP8X4), lhsT_scale=lhs_scales[:, cols],
+                rhs=rhs_words.bitcast(FP8X4), rhs_scale=rhs_scales, start=True, stop=True,
+            )
+
+        x_s = scale_tile("x_s", T, nc.gpsimd)
+        load_scales(nc.scalar, x_s, x_scales, SCALE_ROWS)
+        w1_s = scale_tile("w1_s", H, nc.vector)
+        d_s = scale_tile("d_s", G, nc.gpsimd)
+        load_scales(nc.gpsimd, d_s, d_scales, KEY_SCALE_ROWS)
         key_s = scale_tile("key_s", H, nc.vector)
-        w2s = scale_tile("w2s", N, nc.vector)
+        w2_s = scale_tile("w2_s", N, nc.vector)
 
         offs_t = load_list("offs_t", offs)
-        xw = sb("xw", [P, T], I32)
-        nc.sync.dma_start(xw[:], words_view(x_words))
-        load_scales(nc.sync, xs, x_scales, (0, 1, 2, 3))
-        w1w = sb("w1w", [P, H], I32)
-        nc.sync.dma_start(w1w[:], words_view(w1_words))
-        load_scales(nc.sync, w1s, w1_scales, (0, 1, 2, 3))
+        x_w = load_words("x_w", x_words, T)
+        w1_w = load_words("w1_w", w1_words, H)
+        load_scales(nc.sync, w1_s, w1_scales, SCALE_ROWS)
         n1_t = load_list("n1_t", n1)
         kidx_t = load_list("kidx_t", kidx)
-        gs_t = sb("gs_t", [P, PACK], F32)
-        nc.sync.dma_start(gs_t[:], gs.rearrange("(p t) o -> p (t o)", t=PACK))
+        gs_t = load_gain("gs_t", gs)
         n2_t = load_list("n2_t", n2)
-        dw = sb("dw", [P, G], I32)
-        nc.sync.dma_start(dw[:], words_view(d_words))
+        d_w = load_words("d_w", d_words, G)
         n3_t = load_list("n3_t", n3)
-        gn_t = sb("gn_t", [P, PACK], F32)
-        nc.sync.dma_start(gn_t[:], gn.rearrange("(p t) o -> p (t o)", t=PACK))
-        load_scales(nc.sync, w2s, w2_scales, (0, 1, 2, 3))
+        gn_t = load_gain("gn_t", gn)
+        load_scales(nc.sync, w2_s, w2_scales, SCALE_ROWS)
 
-        warm = sb("warm", [P, 8], F32)
         warm_in = sb("warm_in", [P, 8], F32)
-        nc.gpsimd.memset(warm_in[:], 0.0)
-        nc.scalar.activation(warm[:], warm_in[:], ACT.Sigmoid)
+        warm_out = sb("warm_out", [P, 8], F32)
+        nc.vector.memset(warm_in[:], 0.0)
+        nc.scalar.activation(warm_out[:], warm_in[:], ACT.Sigmoid)
 
-        xq_s = sb("xq_s", [P, S], U8)
-        nc.vector.tensor_copy(xq_s[:], xs[:].indirect(offs_t[:]))
-        xq_w = sb("xq_w", [P, S], U32)
-        nc.vector.tensor_copy(xq_w[:], xw[:].bitcast(U32).indirect(offs_t[:]))
-        w1w_d = sb("w1w_d", [P, H], I32)
-        deal(nc.vector, w1w_d[:], w1w[:], 4)
-        w1s_d = sb("w1s_d", [P, H], U8)
-        deal(nc.vector, w1s_d[:], w1s[:], 16)
+        token_s = sb("token_s", [P, S], U8)
+        nc.vector.tensor_copy(token_s[:], x_s[:].indirect(offs_t[:]))
+        token_w = sb("token_w", [P, S], U32)
+        nc.vector.tensor_copy(token_w[:], x_w[:].bitcast(U32).indirect(offs_t[:]))
+        w1_w_dealt = sb("w1_w_dealt", [P, H], I32)
+        deal(nc.vector, w1_w_dealt[:], w1_w[:], LINE // 4)
+        w1_s_dealt = sb("w1_s_dealt", [P, H], U8)
+        deal(nc.vector, w1_s_dealt[:], w1_s[:], LINE)
 
-        mem_rows = mem.rearrange("(p t) w -> p t w", t=PACK)
         page = []
-        for t, freed in enumerate(("xs", "xw", "w1w", "w1s")):
-            page.append(sb(freed, [P, U], F32))
-            nc.sync.dma_start(page[t][:], mem_rows[:, t, :])
-
-        def product(bank, lw, ls, t, rw, rs):
-            cols = slice(t * P, (t + 1) * P)
-            nc.tensor.matmul_mx(out=bank, lhsT=lw[:, cols].bitcast(FP8X4), lhsT_scale=ls[:, cols],
-                                rhs=rw.bitcast(FP8X4), rhs_scale=rs, start=True, stop=True)
+        for t, freed in enumerate(("x_s", "x_w", "w1_w", "w1_s")):
+            page.append(sb("page%d" % t, [P, U], F32, after=freed))
+            nc.sync.dma_start(page[t][:], planes_view(mem)[:, t, :])
 
         y_banks = []
-        for t in range(PACK):
-            bank = psum.tile([P, S], F32, name="bank")
-            product(bank[:], w1w_d, w1s_d, t, xq_w[:], xq_s[:])
-            y_banks.append(bank)
+        for t in range(PLANES):
+            y_banks.append(psum.tile([P, S], F32, name="bank"))
+            product(y_banks[t][:], w1_w_dealt, w1_s_dealt, t, token_w[:], token_s[:])
 
-        y = [sb("y%d" % t, [P, S], F32) for t in range(PACK)]
-        z = [sb("z%d" % h, [P, HALF * PACK], BF16) for h in range(2)]
-        z_w = sb("z_w", [P, S], U32)
-        z_s = sb("z_s", [P, S], U8)
         halves = [slice(h * HALF, (h + 1) * HALF) for h in range(2)]
-        entries = [slice(h * HALF // 16, (h + 1) * HALF // 16) for h in range(2)]
-
-        a = [sb("a%d" % t, [P, S], F32) for t in range(PACK)]
-        gate = [[sb("gate%d_%d" % (h, t), [P, HALF], F32) for t in range(PACK)] for h in range(2)]
-        far = sb("far", [P, PACK, HALF], F32)
-        near = sb("near", [P, PACK, HALF], F32)
+        y = [sb("y%d" % t, [P, S], F32) for t in range(PLANES)]
+        a = [sb("a%d" % t, [P, S], F32) for t in range(PLANES)]
+        gate = [[sb("gate%d_%d" % (h, t), [P, HALF], F32) for t in range(PLANES)] for h in range(2)]
+        far = sb("far", [P, PLANES, HALF], F32)
+        near = sb("near", [P, PLANES, HALF], F32)
+        z = [sb("z%d" % h, [P, HALF * PLANES], BF16) for h in range(2)]
 
         def make_gate(t, h):
-            nc.scalar.activation(gate[h][t][:], y[t][:].indirect(n1_t[:, entries[h]]), ACT.Sigmoid)
+            nc.scalar.activation(gate[h][t][:], y[t][:].indirect(entries(n1_t, halves[h])), ACT.Sigmoid)
 
-        for t in range(PACK):
+        for t in range(PLANES):
             nc.scalar.copy(y[t][:], y_banks[t][:])
             make_gate(t, 0)
             nc.scalar.activation(a[t][:], y_banks[t][:], ACT.Copy, scale=gs_t[:, t : t + 1])
-            nc.vector.tensor_tensor(far[:, t, :], a[t][:].indirect(n2_t[:, entries[0]]), gate[0][t][:], ALU.mult)
+            nc.vector.tensor_tensor(far[:, t, :], a[t][:].indirect(entries(n2_t, halves[0])), gate[0][t][:], ALU.mult)
             nc.vector.scalar_tensor_tensor(near[:, t, :], gate[0][t][:], 1.0, a[t][:, halves[0]], ALU.subtract, ALU.mult)
 
-        key_s_g = sb("key_s_g", [P, H], U8)
-        nc.vector.tensor_copy(key_s_g[:], ds[:].indirect(kidx_t[:]))
-        key_s_d = sb("key_s_d", [P, H], U8)
-        deal(nc.vector, key_s_d[:], key_s_g[:], 16)
-        key_w_g = sb("key_w_g", [P, H], U32)
-        nc.vector.tensor_copy(key_w_g[:], dw[:].bitcast(U32).indirect(kidx_t[:]))
+        key_s_picked = sb("key_s_picked", [P, H], U8)
+        nc.vector.tensor_copy(key_s_picked[:], d_s[:].indirect(kidx_t[:]))
+        key_s_dealt = sb("key_s_dealt", [P, H], U8)
+        deal(nc.vector, key_s_dealt[:], key_s_picked[:], LINE)
+        key_w_picked = sb("key_w_picked", [P, H], U32)
+        nc.vector.tensor_copy(key_w_picked[:], d_w[:].bitcast(U32).indirect(kidx_t[:]))
         key_w = sb("key_w", [P, H], I32)
-        deal(nc.vector, key_w[:], key_w_g[:].bitcast(I32), 4)
-        for r, src in enumerate((0, 1, 16, 17)):
-            nc.gpsimd.dma_start(key_s[r:P:32, :].bitcast(I32), key_s_d[src:P:32, :].bitcast(I32))
+        deal(nc.vector, key_w[:], key_w_picked[:].bitcast(I32), LINE // 4)
+        for place, picked in zip(SCALE_ROWS, KEY_SCALE_ROWS):
+            nc.sync.dma_start(key_s[place:P:QUADRANT, :].bitcast(I32), key_s_dealt[picked:P:QUADRANT, :].bitcast(I32))
 
-        w2w = sb("ds", [P, N], I32)
-        nc.sync.dma_start(w2w[:], words_view(w2_words))
-        res_t = sb("dw", [P, PACK, U], F32)
-        nc.sync.dma_start(res_t[:], res.rearrange("(p t) w -> p t w", t=PACK))
+        w2_w = load_words("w2_w", w2_words, N, after="d_s")
+        res_t = sb("res_t", [P, PLANES, U], F32, after="key_s_dealt")
+        nc.sync.dma_start(res_t[:], planes_view(res))
 
-        for t in range(PACK):
+        for t in range(PLANES):
             make_gate(t, 1)
         nc.vector.tensor_tensor(
-            z[0][:].rearrange("p (c i t) -> p c t i", t=PACK, i=4),
+            z[0][:].rearrange("p (c i t) -> p c t i", t=PLANES, i=4),
             far[:].rearrange("p t (c i) -> p c t i", i=4),
             near[:].rearrange("p t (c i) -> p c t i", i=4),
             ALU.subtract,
         )
 
-        old_first = sb("old_first", [P, S], F32)
-        old_rest = sb("near", [P, PACK - 1, S], F32)
-        old = [old_first[:]] + [old_rest[:, t, :] for t in range(PACK - 1)]
-        new = [sb("new%d" % t, [P, S], F32) for t in range(PACK)]
-        s_banks = [psum.tile([P, S], F32, name="bank") for t in range(PACK)]
+        s_banks = [psum.tile([P, S], F32, name="bank") for t in range(PLANES)]
+        z_s = [sb("z_s%d" % h, [P, HALF], U8) for h in range(2)]
 
-        def quantise_z(h):
-            nc.vector.quantize_mx(out=z_w[:, halves[h]].bitcast(FP8X4), scales=z_s[:, halves[h]], in_=z[h][:])
+        def score(h, after=None):
+            z_w = sb("z_w%d" % h, [P, HALF], U32, after)
+            nc.vector.quantize_mx(out=z_w[:].bitcast(FP8X4), scales=z_s[h][:], in_=z[h][:])
+            for t in range(PLANES):
+                product(s_banks[t][:, halves[h]], key_w, key_s, t, z_w[:], z_s[h][:])
 
-        def score(t, cols):
-            product(s_banks[t][:, cols], key_w, key_s, t, z_w[:, cols], z_s[:, cols])
-
-        last = PACK - 1
-        for t in range(PACK):
-            nc.vector.tensor_copy(far[:, t, :], a[t][:].indirect(n2_t[:, entries[1]]))
+        for t in range(PLANES):
+            nc.vector.tensor_copy(far[:, t, :], a[t][:].indirect(entries(n2_t, halves[1])))
             if t == 0:
-                quantise_z(0)
-                for u in range(last):
-                    score(u, halves[0])
-
+                score(0)
         for pair in ((0, 1), (2, 3)):
             step = {t: ring.tile([P, HALF], F32, name="step") for t in pair}
             pull = {t: ring.tile([P, HALF], F32, name="pull") for t in pair}
@@ -195,117 +213,93 @@ def tile_picked_pqktrackpagex_none_po_kernel(
                 nc.gpsimd.tensor_tensor(pull[t][:], step[t][:], gate[1][t][:], ALU.mult)
             for t in pair:
                 nc.gpsimd.tensor_tensor(mixed[t][:], pull[t][:], a[t][:, halves[1]], ALU.add)
-                nc.scalar.copy(z[1][:].rearrange("p (j t) -> p t j", t=PACK)[:, t, :], mixed[t][:])
+                nc.scalar.copy(plane_of(z[1], t), mixed[t][:])
 
-        for t in range(PACK):
+        old_first = sb("old_first", [P, S], F32)
+        old_rest = sb("old_rest", [P, PLANES - 1, S], F32, after="near")
+        old = [old_first[:]] + [old_rest[:, t, :] for t in range(PLANES - 1)]
+        new = {}
+        for t in range(PLANES):
             nc.vector.tensor_scalar(old[t], page[t][:].indirect(n3_t[:]), 0.5, 0.0, ALU.mult, ALU.add)
 
-        chunks = []
-        start = 0
-        for width in WIDTHS:
-            chunks.append(slice(start, start + width))
-            start = start + width
-        z2 = [sb("z2_%d" % c, [P, width * PACK], BF16) for c, width in enumerate(WIDTHS)]
-        staged = sum(WIDTHS[:STAGED])
-        z2_planes = sb("z2_planes", [P, PACK, staged], BF16)
+        chunks = [slice(sum(WIDTHS[:c]), sum(WIDTHS[: c + 1])) for c in range(len(WIDTHS))]
+        z2 = [sb("z2_%d" % c, [P, width * PLANES], BF16) for c, width in enumerate(WIDTHS)]
+        z2_planes = sb("z2_planes", [P, PLANES, sum(WIDTHS[:WOVEN])], BF16)
 
         def larger(t, cols):
-            nc.vector.scalar_tensor_tensor(new[t][:, cols], s_banks[t][:, cols], 0.0625, old[t][:, cols], ALU.mult, ALU.max)
+            new[t, cols.start] = sb("new%d_%d" % (t, cols.start), [P, cols.stop - cols.start], F32)
+            nc.vector.scalar_tensor_tensor(new[t, cols.start][:], s_banks[t][:, cols], 0.0625, old[t][:, cols], ALU.mult, ALU.max)
 
         def put(t, cols):
-            nc.vector.tensor_copy(page[t][:].indirect(n3_t[:, cols.start // 16 : cols.stop // 16]), new[t][:, cols])
+            nc.vector.tensor_copy(page[t][:].indirect(entries(n3_t, cols)), new[t, cols.start][:])
 
         def weigh(t):
             for c, cols in enumerate(chunks):
-                if c < STAGED:
-                    dst = z2_planes[:, t, cols]
-                else:
-                    dst = z2[c][:].rearrange("p (w t) -> p t w", t=PACK)[:, t, :]
+                dst = z2_planes[:, t, cols] if c < WOVEN else plane_of(z2[c], t)
                 nc.scalar.activation(dst, page[t][:, cols], ACT.Copy, scale=gn_t[:, t : t + 1])
 
-        whole = slice(0, S)
-        for h in range(2):
-            pieces = [(t, halves[h]) for t in range(last)]
-            if h == 1:
-                pieces.append((last, whole))
-            larger(*pieces[0])
-            for n, (t, cols) in enumerate(pieces):
-                if n + 1 < len(pieces):
-                    larger(*pieces[n + 1])
-                elif h == 0:
-                    quantise_z(1)
-                    for u in range(last):
-                        score(u, halves[1])
-                    score(last, whole)
-                put(t, cols)
-                if h == 1:
-                    weigh(t)
+        last = PLANES - 1
+        larger(0, halves[0])
+        for t in range(last):
+            if t + 1 < last:
+                larger(t + 1, halves[0])
+            else:
+                score(1, after="new1_0")
+            put(t, halves[0])
+        pieces = [(t, halves[1]) for t in range(last)] + [(last, slice(0, S))]
+        larger(*pieces[0])
+        for n, (t, cols) in enumerate(pieces):
+            if n + 1 < len(pieces):
+                larger(*pieces[n + 1])
+            put(t, cols)
+            weigh(t)
 
-        w2w_d = sb("a3", [P, N], I32)
-        deal(nc.gpsimd, w2w_d[:], w2w[:], 4)
-        w2s_d = sb("a2", [P, N], U8)
-        deal(nc.gpsimd, w2s_d[:], w2s[:], 16)
+        w2_w_dealt = sb("w2_w_dealt", [P, N], I32, after="a3")
+        deal(nc.gpsimd, w2_w_dealt[:], w2_w[:], LINE // 4)
+        w2_s_dealt = sb("w2_s_dealt", [P, N], U8, after="a2")
+        deal(nc.gpsimd, w2_s_dealt[:], w2_s[:], LINE)
 
-        probe = sb("probe", [P, 8], F32)
-        nc.gpsimd.tensor_copy(probe[:, 0:1], page[3][:, 0:1])
-        out_rows = out_0.rearrange("(p t) w -> p t w", t=PACK)
-        out_words = words_view(out_1)
         out_s = sb("out_s", [P, U], U8)
-        banks = {}
-        rounded = {}
-
-        def weave(c):
-            if c < STAGED:
-                nc.vector.tensor_copy(
-                    z2[c][:].rearrange("p (c i t) -> p c t i", t=PACK, i=4),
-                    z2_planes[:, :, chunks[c]].rearrange("p t (c i) -> p c t i", i=4),
-                )
+        out_banks, rounded = {}, {}
 
         def multiply(c):
             width = WIDTHS[c]
             z2_w = sb("z2_w%d" % c, [P, width], U32)
             z2_s = sb("z2_s%d" % c, [P, width], U8)
             nc.vector.quantize_mx(out=z2_w[:].bitcast(FP8X4), scales=z2_s[:], in_=z2[c][:])
-            per_bank = 512 // width
-            banks[c] = []
-            for b in range(PACK // per_bank):
+            per_bank = BANK // width
+            out_banks[c] = []
+            for first in range(0, PLANES, per_bank):
                 bank = psum.tile([P, per_bank, width], F32, name="bank")
                 for u in range(per_bank):
-                    product(bank[:, u, :], w2w_d, w2s_d, per_bank * b + u, z2_w[:], z2_s[:])
-                banks[c].append(bank)
+                    product(bank[:, u, :], w2_w_dealt, w2_s_dealt, first + u, z2_w[:], z2_s[:])
+                out_banks[c].append((slice(first, first + per_bank), bank))
 
-        def finish(c):
-            width = WIDTHS[c]
-            cols = chunks[c]
-            per_bank = 512 // width
-            result = sb("result%d" % c, [P, PACK, width], F32)
-            for b, bank in enumerate(banks[c]):
-                planes = slice(per_bank * b, per_bank * (b + 1))
-                nc.vector.tensor_tensor(result[:, planes, :], bank[:], res_t[:, planes, cols], ALU.add)
-            nc.sync.dma_start(out_rows[:, :, cols], result[:])
-            rounded[c] = sb("rounded%d" % c, [P, width * PACK], BF16)
-            nc.scalar.copy(
-                rounded[c][:].rearrange("p (c i t) -> p c t i", t=PACK, i=4),
-                result[:].rearrange("p t (c i) -> p c t i", i=4),
-            )
+        def add_residual(c):
+            result = sb("result%d" % c, [P, PLANES, WIDTHS[c]], F32)
+            for planes, bank in out_banks[c]:
+                nc.vector.tensor_tensor(result[:, planes, :], bank[:], res_t[:, planes, chunks[c]], ALU.add)
+            nc.sync.dma_start(planes_view(out_0)[:, :, chunks[c]], result[:])
+            rounded[c] = sb("rounded%d" % c, [P, WIDTHS[c] * PLANES], BF16)
+            interleave(nc.scalar.copy, rounded[c][:], result[:])
 
         def hand_on(c):
             out_w = sb("out_w%d" % c, [P, WIDTHS[c]], I32)
             nc.vector.quantize_mx(out=out_w[:].bitcast(FP8X4), scales=out_s[:, chunks[c]], in_=rounded[c][:])
-            nc.sync.dma_start(out_words[:, chunks[c]], out_w[:])
+            nc.sync.dma_start(words_view(out_1)[:, chunks[c]], out_w[:])
 
         count = len(WIDTHS)
-        weave(0)
-        for step in range(count + 2):
-            if step + 1 < count:
-                weave(step + 1)
-            if step < count:
-                multiply(step)
-            if 0 <= step - 1 < count:
-                finish(step - 1)
-            if 0 <= step - 2 < count:
-                hand_on(step - 2)
+        for turn in range(-1, count + 2):
+            if turn + 1 < WOVEN:
+                interleave(nc.vector.tensor_copy, z2[turn + 1][:], z2_planes[:, :, chunks[turn + 1]])
+            if 0 <= turn < count:
+                multiply(turn)
+            if 0 <= turn - 1 < count:
+                add_residual(turn - 1)
+            if 0 <= turn - 2 < count:
+                hand_on(turn - 2)
+
         scale_rows = out_2[0].bitcast(I32)
-        for q in range(4):
+        for q in range(P // QUADRANT):
             queue = nc.sync if q % 2 == 0 else nc.scalar
-            queue.dma_start(scale_rows[4 * q : 4 * q + 4, :], out_s[32 * q : 32 * q + 4, :].bitcast(I32))
+            queue.dma_start(scale_rows[4 * q : 4 * q + 4, :], out_s[QUADRANT * q : QUADRANT * q + 4, :].bitcast(I32))

from contextlib import ExitStack

import concourse.mybir as mybir

K, T, S, N, H, G, U = 512, 1024, 512, 512, 512, 2048, 1024
FLOPS = 2 * K * H * S + 2 * K * H * S + 2 * H * N * U

F32 = mybir.dt.float32
BF16 = mybir.dt.bfloat16
I32 = mybir.dt.int32
U32 = mybir.dt.uint32
U16 = mybir.dt.uint16
U8 = mybir.dt.uint8
FP8X4 = mybir.dt.float8_e4m3fn_x4
ALU = mybir.AluOpType
ACT = mybir.ActivationFunctionType

P = 128
PLANES = 4
GROUP = 16
QUADRANT = 32
BANK = 512
LINE = 16
HALF = S // 2
WIDTHS = (256, 256, 256, 128, 128)
WOVEN = 2
SCALE_ROWS = (0, 1, 2, 3)
KEY_SCALE_ROWS = (0, 1, GROUP, GROUP + 1)


def words_view(words):
    return words[0].rearrange("p n t -> p (n t)").bitcast(I32)


def planes_view(rows):
    return rows.rearrange("(p t) w -> p t w", t=PLANES)


def deal(engine, dst, src, per_line):
    engine.tensor_copy(
        out=dst.rearrange("p (t c i) -> p c t i", t=PLANES, i=per_line),
        in_=src.rearrange("p (c i t) -> p c t i", t=PLANES, i=per_line),
    )


def interleave(copy, dst, src):
    copy(
        dst.rearrange("p (c i t) -> p c t i", t=PLANES, i=4),
        src.rearrange("p t (c i) -> p c t i", i=4),
    )


def plane_of(interleaved, t):
    return interleaved[:].rearrange("p (c t) -> p t c", t=PLANES)[:, t, :]


def entries(lists, cols):
    return lists[:, cols.start // GROUP : cols.stop // GROUP]


def tile_picked_pqktrackpagex_none_po_kernel(
    tc, x_words, x_scales, w1_words, w1_scales, gs, d_words, d_scales, mem, res, gn, w2_words, w2_scales,
    offs, n1, n2, kidx, n3, out_0, out_1, out_2,
):
    nc = tc.nc
    with ExitStack() as ctx:
        keep = ctx.enter_context(tc.tile_pool(name="keep", bufs=1))
        ring = ctx.enter_context(tc.tile_pool(name="ring", bufs=PLANES))
        psum = ctx.enter_context(tc.psum_pool(name="psum", bufs=8))

        def sb(name, shape, dtype, after=None):
            return keep.tile(shape, dtype, name=name, tag=after or name, align_bytes=64)

        def load_list(name, src):
            lists = keep.tile([P, S // GROUP], U16, name=name)
            nc.sync.dma_start(lists[:], src)
            return lists

        def load_words(name, src, width, after=None):
            words = sb(name, [P, width], I32, after)
            nc.sync.dma_start(words[:], words_view(src))
            return words

        def load_gain(name, src):
            gain = sb(name, [P, PLANES], F32)
            nc.sync.dma_start(gain[:], src.rearrange("(p t) o -> p (t o)", t=PLANES))
            return gain

        def scale_tile(name, width, engine):
            scales = sb(name, [P, width], U8)
            engine.memset(scales[:].bitcast(I32), 0)
            return scales

        def load_scales(queue, scales, src, first_partitions):
            rows = src[0].bitcast(I32)
            for r, first in enumerate(first_partitions):
                queue.dma_start(scales[first:P:QUADRANT, :].bitcast(I32), rows[r :: len(first_partitions), :])

        def product(bank, lhs_words, lhs_scales, t, rhs_words, rhs_scales):
            cols = slice(t * P, (t + 1) * P)
            nc.tensor.matmul_mx(
                out=bank, lhsT=lhs_words[:, cols].bitcast(FP8X4), lhsT_scale=lhs_scales[:, cols],
                rhs=rhs_words.bitcast(FP8X4), rhs_scale=rhs_scales, start=True, stop=True,
            )

        x_s = scale_tile("x_s", T, nc.gpsimd)
        load_scales(nc.scalar, x_s, x_scales, SCALE_ROWS)
        w1_s = scale_tile("w1_s", H, nc.vector)
        d_s = scale_tile("d_s", G, nc.gpsimd)
        load_scales(nc.gpsimd, d_s, d_scales, KEY_SCALE_ROWS)
        key_s = scale_tile("key_s", H, nc.vector)
        w2_s = scale_tile("w2_s", N, nc.vector)

        offs_t = load_list("offs_t", offs)
        x_w = load_words("x_w", x_words, T)
        w1_w = load_words("w1_w", w1_words, H)
        load_scales(nc.sync, w1_s, w1_scales, SCALE_ROWS)
        n1_t = load_list("n1_t", n1)
        kidx_t = load_list("kidx_t", kidx)
        gs_t = load_gain("gs_t", gs)
        n2_t = load_list("n2_t", n2)
        d_w = load_words("d_w", d_words, G)
        n3_t = load_list("n3_t", n3)
        gn_t = load_gain("gn_t", gn)
        load_scales(nc.sync, w2_s, w2_scales, SCALE_ROWS)

        warm_in = sb("warm_in", [P, 8], F32)
        warm_out = sb("warm_out", [P, 8], F32)
        nc.vector.memset(warm_in[:], 0.0)
        nc.scalar.activation(warm_out[:], warm_in[:], ACT.Sigmoid)

        token_s = sb("token_s", [P, S], U8)
        nc.vector.tensor_copy(token_s[:], x_s[:].indirect(offs_t[:]))
        token_w = sb("token_w", [P, S], U32)
        nc.vector.tensor_copy(token_w[:], x_w[:].bitcast(U32).indirect(offs_t[:]))
        w1_w_dealt = sb("w1_w_dealt", [P, H], I32)
        deal(nc.vector, w1_w_dealt[:], w1_w[:], LINE // 4)
        w1_s_dealt = sb("w1_s_dealt", [P, H], U8)
        deal(nc.vector, w1_s_dealt[:], w1_s[:], LINE)

        page = []
        for t, freed in enumerate(("x_s", "x_w", "w1_w", "w1_s")):
            page.append(sb("page%d" % t, [P, U], F32, after=freed))
            nc.sync.dma_start(page[t][:], planes_view(mem)[:, t, :])

        y_banks = []
        for t in range(PLANES):
            y_banks.append(psum.tile([P, S], F32, name="bank"))
            product(y_banks[t][:], w1_w_dealt, w1_s_dealt, t, token_w[:], token_s[:])

        halves = [slice(h * HALF, (h + 1) * HALF) for h in range(2)]
        y = [sb("y%d" % t, [P, S], F32) for t in range(PLANES)]
        a = [sb("a%d" % t, [P, S], F32) for t in range(PLANES)]
        gate = [[sb("gate%d_%d" % (h, t), [P, HALF], F32) for t in range(PLANES)] for h in range(2)]
        far = sb("far", [P, PLANES, HALF], F32)
        near = sb("near", [P, PLANES, HALF], F32)
        z = [sb("z%d" % h, [P, HALF * PLANES], BF16) for h in range(2)]

        def make_gate(t, h):
            nc.scalar.activation(gate[h][t][:], y[t][:].indirect(entries(n1_t, halves[h])), ACT.Sigmoid)

        for t in range(PLANES):
            nc.scalar.copy(y[t][:], y_banks[t][:])
            make_gate(t, 0)
            nc.scalar.activation(a[t][:], y_banks[t][:], ACT.Copy, scale=gs_t[:, t : t + 1])
            nc.vector.tensor_tensor(far[:, t, :], a[t][:].indirect(entries(n2_t, halves[0])), gate[0][t][:], ALU.mult)
            nc.vector.scalar_tensor_tensor(near[:, t, :], gate[0][t][:], 1.0, a[t][:, halves[0]], ALU.subtract, ALU.mult)

        key_s_picked = sb("key_s_picked", [P, H], U8)
        nc.vector.tensor_copy(key_s_picked[:], d_s[:].indirect(kidx_t[:]))
        key_s_dealt = sb("key_s_dealt", [P, H], U8)
        deal(nc.vector, key_s_dealt[:], key_s_picked[:], LINE)
        key_w_picked = sb("key_w_picked", [P, H], U32)
        nc.vector.tensor_copy(key_w_picked[:], d_w[:].bitcast(U32).indirect(kidx_t[:]))
        key_w = sb("key_w", [P, H], I32)
        deal(nc.vector, key_w[:], key_w_picked[:].bitcast(I32), LINE // 4)
        for place, picked in zip(SCALE_ROWS, KEY_SCALE_ROWS):
            nc.sync.dma_start(key_s[place:P:QUADRANT, :].bitcast(I32), key_s_dealt[picked:P:QUADRANT, :].bitcast(I32))

        w2_w = load_words("w2_w", w2_words, N, after="d_s")
        res_t = sb("res_t", [P, PLANES, U], F32, after="key_s_dealt")
        nc.sync.dma_start(res_t[:], planes_view(res))

        for t in range(PLANES):
            make_gate(t, 1)
        nc.vector.tensor_tensor(
            z[0][:].rearrange("p (c i t) -> p c t i", t=PLANES, i=4),
            far[:].rearrange("p t (c i) -> p c t i", i=4),
            near[:].rearrange("p t (c i) -> p c t i", i=4),
            ALU.subtract,
        )

        s_banks = [psum.tile([P, S], F32, name="bank") for t in range(PLANES)]
        z_s = [sb("z_s%d" % h, [P, HALF], U8) for h in range(2)]

        def score(h, after=None):
            z_w = sb("z_w%d" % h, [P, HALF], U32, after)
            nc.vector.quantize_mx(out=z_w[:].bitcast(FP8X4), scales=z_s[h][:], in_=z[h][:])
            for t in range(PLANES):
                product(s_banks[t][:, halves[h]], key_w, key_s, t, z_w[:], z_s[h][:])

        for t in range(PLANES):
            nc.vector.tensor_copy(far[:, t, :], a[t][:].indirect(entries(n2_t, halves[1])))
            if t == 0:
                score(0)
        for pair in ((0, 1), (2, 3)):
            step = {t: ring.tile([P, HALF], F32, name="step") for t in pair}
            pull = {t: ring.tile([P, HALF], F32, name="pull") for t in pair}
            mixed = {t: ring.tile([P, HALF], F32, name="mixed") for t in pair}
            for t in pair:
                nc.gpsimd.tensor_tensor(step[t][:], far[:, t, :], a[t][:, halves[1]], ALU.subtract)
            for t in pair:
                nc.gpsimd.tensor_tensor(pull[t][:], step[t][:], gate[1][t][:], ALU.mult)
            for t in pair:
                nc.gpsimd.tensor_tensor(mixed[t][:], pull[t][:], a[t][:, halves[1]], ALU.add)
                nc.scalar.copy(plane_of(z[1], t), mixed[t][:])

        old_first = sb("old_first", [P, S], F32)
        old_rest = sb("old_rest", [P, PLANES - 1, S], F32, after="near")
        old = [old_first[:]] + [old_rest[:, t, :] for t in range(PLANES - 1)]
        new = {}
        for t in range(PLANES):
            nc.vector.tensor_scalar(old[t], page[t][:].indirect(n3_t[:]), 0.5, 0.0, ALU.mult, ALU.add)

        chunks = [slice(sum(WIDTHS[:c]), sum(WIDTHS[: c + 1])) for c in range(len(WIDTHS))]
        z2 = [sb("z2_%d" % c, [P, width * PLANES], BF16) for c, width in enumerate(WIDTHS)]
        z2_planes = sb("z2_planes", [P, PLANES, sum(WIDTHS[:WOVEN])], BF16)

        def larger(t, cols):
            new[t, cols.start] = sb("new%d_%d" % (t, cols.start), [P, cols.stop - cols.start], F32)
            nc.vector.scalar_tensor_tensor(new[t, cols.start][:], s_banks[t][:, cols], 0.0625, old[t][:, cols], ALU.mult, ALU.max)

        def put(t, cols):
            nc.vector.tensor_copy(page[t][:].indirect(entries(n3_t, cols)), new[t, cols.start][:])

        def weigh(t):
            for c, cols in enumerate(chunks):
                dst = z2_planes[:, t, cols] if c < WOVEN else plane_of(z2[c], t)
                nc.scalar.activation(dst, page[t][:, cols], ACT.Copy, scale=gn_t[:, t : t + 1])

        last = PLANES - 1
        larger(0, halves[0])
        for t in range(last):
            if t + 1 < last:
                larger(t + 1, halves[0])
            else:
                score(1, after="new1_0")
            put(t, halves[0])
        pieces = [(t, halves[1]) for t in range(last)] + [(last, slice(0, S))]
        larger(*pieces[0])
        for n, (t, cols) in enumerate(pieces):
            if n + 1 < len(pieces):
                larger(*pieces[n + 1])
            put(t, cols)
            weigh(t)

        w2_w_dealt = sb("w2_w_dealt", [P, N], I32, after="a3")
        deal(nc.gpsimd, w2_w_dealt[:], w2_w[:], LINE // 4)
        w2_s_dealt = sb("w2_s_dealt", [P, N], U8, after="a2")
        deal(nc.gpsimd, w2_s_dealt[:], w2_s[:], LINE)

        out_s = sb("out_s", [P, U], U8)
        out_banks, rounded = {}, {}

        def multiply(c):
            width = WIDTHS[c]
            z2_w = sb("z2_w%d" % c, [P, width], U32)
            z2_s = sb("z2_s%d" % c, [P, width], U8)
            nc.vector.quantize_mx(out=z2_w[:].bitcast(FP8X4), scales=z2_s[:], in_=z2[c][:])
            per_bank = BANK // width
            out_banks[c] = []
            for first in range(0, PLANES, per_bank):
                bank = psum.tile([P, per_bank, width], F32, name="bank")
                for u in range(per_bank):
                    product(bank[:, u, :], w2_w_dealt, w2_s_dealt, first + u, z2_w[:], z2_s[:])
                out_banks[c].append((slice(first, first + per_bank), bank))

        def add_residual(c):
            result = sb("result%d" % c, [P, PLANES, WIDTHS[c]], F32)
            for planes, bank in out_banks[c]:
                nc.vector.tensor_tensor(result[:, planes, :], bank[:], res_t[:, planes, chunks[c]], ALU.add)
            nc.sync.dma_start(planes_view(out_0)[:, :, chunks[c]], result[:])
            rounded[c] = sb("rounded%d" % c, [P, WIDTHS[c] * PLANES], BF16)
            interleave(nc.scalar.copy, rounded[c][:], result[:])

        def hand_on(c):
            out_w = sb("out_w%d" % c, [P, WIDTHS[c]], I32)
            nc.vector.quantize_mx(out=out_w[:].bitcast(FP8X4), scales=out_s[:, chunks[c]], in_=rounded[c][:])
            nc.sync.dma_start(words_view(out_1)[:, chunks[c]], out_w[:])

        count = len(WIDTHS)
        for turn in range(-1, count + 2):
            if turn + 1 < WOVEN:
                interleave(nc.vector.tensor_copy, z2[turn + 1][:], z2_planes[:, :, chunks[turn + 1]])
            if 0 <= turn < count:
                multiply(turn)
            if 0 <= turn - 1 < count:
                add_residual(turn - 1)
            if 0 <= turn - 2 < count:
                hand_on(turn - 2)

        scale_rows = out_2[0].bitcast(I32)
        for q in range(P // QUADRANT):
            queue = nc.sync if q % 2 == 0 else nc.scalar
            queue.dma_start(scale_rows[4 * q : 4 * q + 4, :], out_s[QUADRANT * q : QUADRANT * q + 4, :].bitcast(I32))
